import numpy as np
import ml_dtypes


def mxq(x, axis, fmt="e4m3"):
    dtype, down = {"e4m3": (ml_dtypes.float8_e4m3fn, 7), "e5m2": (ml_dtypes.float8_e5m2, 14)}[fmt]
    v = np.moveaxis(np.asarray(x, np.float32).astype(ml_dtypes.bfloat16).astype(np.float64), axis, -1)
    blocks = v.reshape(v.shape[:-1] + (-1, 32))
    amax = np.abs(blocks).max(-1, keepdims=True)
    byte = np.maximum(np.where(amax > 0, np.frexp(amax)[1] - 1 + 127, 0) - down, 1)
    scale = np.exp2(byte - 127.0)
    codes = (blocks / scale).astype(np.float32).astype(dtype).astype(np.float64)
    return np.moveaxis((codes * scale).reshape(v.shape), -1, axis)


WIDE = False


def mx_kscale(k):
    if not WIDE:
        return np.ones(k)
    levels = np.array([10, -10, 5, -5, 0])
    if k % 512:
        return np.exp2(np.random.permutation(np.resize(levels, k // 32))).repeat(32)
    a = np.empty((k // 512, 16))
    for p in range(k // 512):
        a[p, :8] = np.random.permutation(np.resize(levels, 8))
        for g in range(8):
            far = levels[np.abs(levels - a[p, g]) >= 10]
            a[p, g + 8] = far[np.random.randint(len(far))]
    return np.exp2(a.ravel()).repeat(32)


def f64(x):
    return np.asarray(x).astype(np.float64)


def striped(idx):
    return np.tile(idx.reshape(-1, 16).T, (8, 1)).astype(np.uint16)


def unstriped(offs):
    return offs[:16].T.reshape(-1).astype(np.int64)


E2M1 = np.array([0.0, 0.5, 1.0, 1.5, 2.0, 3.0, 4.0, 6.0, -0.0, -0.5, -1.0, -1.5, -2.0, -3.0, -4.0, -6.0])


def pack_weight(w, fmt):
    k, n = w.shape
    w = f64(np.asarray(w, np.float32).astype(ml_dtypes.bfloat16)).reshape(k // 32, 32, n)
    amax = np.abs(w).max(1)
    if fmt == "e4m3":
        byte = np.frexp(amax)[1] - 1 + 127 - 7
    else:
        mant, ex = np.frexp(amax / 6.0)
        byte = np.where(mant > 0.5, ex, ex - 1) + 127
    byte = np.clip(np.where(amax > 0, byte, 1), 1, 254)
    scaled = (w * np.exp2(127.0 - byte)[:, None, :]).reshape(k, n).astype(np.float32)
    by_word = np.ascontiguousarray(scaled.reshape(k // 512, 128, 4, n).transpose(0, 1, 3, 2))
    if fmt == "e4m3":
        words = by_word.astype(ml_dtypes.float8_e4m3fn).view(np.uint8)
    else:
        c = by_word.astype(ml_dtypes.float4_e2m1fn).view(np.uint8) & 0xF
        words = (c[..., 0::2] | (c[..., 1::2] << 4)).reshape(k // 512, 128, 2 * n)
    return np.ascontiguousarray(words), np.ascontiguousarray(byte.astype(np.uint8).reshape(k // 512, 16, n))


def unpack_weight(words, scales, fmt):
    g, _, n = scales.shape
    words = np.ascontiguousarray(words).reshape(g, 128, n, -1)
    if fmt == "e4m3":
        vals = words.view(ml_dtypes.float8_e4m3fn).astype(np.float64)
    else:
        nib = np.empty((g, 128, n, 4), np.uint8)
        nib[..., 0::2] = words & 0xF
        nib[..., 1::2] = words >> 4
        vals = E2M1[nib]
    vals = vals * np.repeat(np.exp2(scales.astype(np.float64) - 127.0), 8, axis=1)[..., None]
    return vals.transpose(0, 1, 3, 2).reshape(g * 512, n)


def gelu(v):
    return 0.5 * v * (1.0 + np.tanh(np.sqrt(2.0 / np.pi) * (v + 0.044715 * v**3)))


K, H, T, S, T3, S2, P = 1536, 512, 2048, 1024, 2048, 1024, 512


def setup_inputs():
    n = np.random.standard_normal
    s = mx_kscale(K)[:, None]
    u = mx_kscale(H)[:, None]
    d = {}
    d["tab_words"], d["tab_scales"] = pack_weight(n((K, T)) * s, "e4m3")
    d["tab2_words"], d["tab2_scales"] = pack_weight(n((H, T3)) / H ** 0.5 / u, "e4m3")
    d["offs"] = striped(np.random.permutation(T)[:S])
    d["offs2"] = striped(np.random.permutation(T3)[:S2])
    d["pos1"] = striped(np.random.permutation(S)[:P])
    d["pos2"] = striped(np.random.permutation(S)[:P])
    d["w1"] = (n((K, H)) / K ** 0.5 / s).astype(np.float32)
    d["w4_words"], d["w4_scales"] = pack_weight(n((K, H)) / K ** 0.5 / s * u.T, "e2m1")
    d["wave"] = (0.8 * n((H, S))).astype(np.float32)
    d["gain"] = (0.5 * np.exp(0.3 * n(H)) * u[:, 0]).astype(np.float32)
    d["rider"] = (1.2 * n((S2, P))).astype(np.float32)
    d["hull"] = n(S2).astype(np.float32)
    return d


def reference(tab_words, tab_scales, tab2_words, tab2_scales, offs, offs2, pos1, pos2,
              w1, w4_words, w4_scales, wave, gain, rider, hull):
    v = unpack_weight(tab_words, tab_scales, "e4m3")[:, unstriped(offs)]
    v2 = unpack_weight(tab2_words, tab2_scales, "e4m3")[:, unstriped(offs2)]
    w4 = unpack_weight(w4_words, w4_scales, "e2m1")
    a = mxq(f64(w1), 0, "e4m3").T @ v
    miss = np.square(a - f64(wave))
    b = w4.T @ v
    h = b - f64(gain)[:, None] * miss
    e = v2.T @ mxq(h, 0, "e4m3")
    takeoff = np.maximum(e[:, unstriped(pos1)], f64(rider))
    turn = np.maximum(e[:, unstriped(pos2)], f64(hull)[:, None])
    return takeoff - turn

@@ -1,0 +1,272 @@
+from contextlib import ExitStack
+
+import concourse.mybir as mybir
+
+K, H, T, S, S2, NP = 1536, 512, 2048, 1024, 1024, 512
+FLOPS = 2 * (2 * K * H * S + H * S2 * S)
+
+F32 = mybir.dt.float32
+BF16 = mybir.dt.bfloat16
+I32 = mybir.dt.int32
+U32 = mybir.dt.uint32
+U16 = mybir.dt.uint16
+U8 = mybir.dt.uint8
+FP8X4 = mybir.dt.float8_e4m3fn_x4
+FP4X4 = mybir.dt.float4_e2m1fn_x4
+ALU = mybir.AluOpType
+ACT = mybir.ActivationFunctionType
+
+P = 128
+PACK = 4
+PASSES = K // (P * PACK)
+BANK = 512
+HALVES = S // BANK
+PIECE = 256
+M_TILES = S2 // P
+FIRST = 256
+SHIFT_ROWS = 112
+
+
+def tile_list_surfboard_blank_scores_kernel(
+    tc, tab_words, tab_scales, tab2_words, tab2_scales, offs, offs2, pos1, pos2,
+    w1, w4_words, w4_scales, wave, gain, rider, hull, out,
+):
+    nc = tc.nc
+    with ExitStack() as ctx:
+        keep = ctx.enter_context(tc.tile_pool(name="keep", bufs=1))
+        ring = ctx.enter_context(tc.tile_pool(name="ring", bufs=3))
+        psum = ctx.enter_context(tc.psum_pool(name="psum", bufs=8))
+
+        def held(shape, dtype, name, tag=None):
+            return keep.tile(shape, dtype, name=name, tag=tag or name, align_bytes=64)
+
+        offs_t = held([P, S // 16], U16, "offs_t")
+        offs2_t = held([P, S2 // 16], U16, "offs2_t")
+        pos1_t = held([P, NP // 16], U16, "pos1_t")
+        pos2_t = held([P, NP // 16], U16, "pos2_t")
+
+        tab_w = [held([P, T], I32, "tab_w%d" % a) for a in range(PASSES)]
+        tab_s = held([P, T], U8, "tab_s")
+        tab2_w = held([P, T], I32, "tab2_w")
+        tab2_s = held([P, T], U8, "tab2_s")
+        w1_raw = [held([P, PACK, H], F32, "w1_raw%d" % a) for a in range(PASSES)]
+        w4_raw = held([P, PASSES, 2 * H], U8, "w4_raw")
+        w4s_raw = held([P, PASSES, H], U8, "w4s_raw")
+        wave_t = [[held([P, 2, BANK], F32, "wave%d_%d" % (jh, u)) for u in range(2)] for jh in range(HALVES)]
+        rider_t = [held([P, 2, NP], F32, "rider%d" % u) for u in range(M_TILES // 2)]
+        gain_t = held([P, PACK], F32, "gain_t")
+        hull_t = held([P, M_TILES], F32, "hull_t")
+        v_s = held([P, S], U8, "v_s")
+        v_s0 = [v_s] + [held([P, S], U8, "v_s%d" % a) for a in range(1, PASSES)]
+
+        nc.gpsimd.memset(tab_s[:].bitcast(I32), 0)
+        nc.gpsimd.memset(w4s_raw[:].rearrange("p a c -> p (a c)").bitcast(I32), 0)
+        for plane in (tab2_s, v_s0[1], v_s0[2]):
+            nc.vector.memset(plane[:].bitcast(I32), 0)
+
+        def load_words(dst, words):
+            nc.sync.dma_start(dst[:], words.rearrange("p t i -> p (t i)").bitcast(I32))
+
+        def load_w1(a):
+            rows = w1[a * P * PACK : (a + 1) * P * PACK, :]
+            nc.sync.dma_start(w1_raw[a][:], rows.rearrange("(p i) r -> p i r", i=PACK))
+
+        def load_wave(jh, u):
+            src = wave.rearrange("(p t) j -> p t j", t=PACK)
+            nc.sync.dma_start(wave_t[jh][u][:], src[:, 2 * u : 2 * u + 2, jh * BANK : (jh + 1) * BANK])
+
+        nc.sync.dma_start(offs_t[:], offs)
+        nc.sync.dma_start(w4_raw[:].bitcast(I32), w4_words.rearrange("a p c -> p a c").bitcast(I32))
+        load_words(tab_w[0], tab_words[0])
+        for q in range(4):
+            nc.sync.dma_start(
+                tab_s[32 * q : 32 * q + 4 * PASSES, :].bitcast(I32),
+                tab_scales[:, 4 * q : 4 * q + 4, :].bitcast(I32),
+            )
+        warm = held([P, 1], F32, "warm")
+        nc.vector.memset(warm[:], 0.0)
+        warm2 = held([P, 1], F32, "warm2")
+        nc.scalar.activation(warm2[:], warm[:], ACT.Square)
+        load_w1(0)
+        load_w1(1)
+        load_w1(2)
+        for q in range(4):
+            nc.sync.dma_start(
+                w4s_raw[32 * q : 32 * q + 4, :, :].bitcast(I32),
+                w4_scales[:, 4 * q : 4 * q + 4, :].rearrange("a q c -> q a c").bitcast(I32),
+            )
+        load_words(tab_w[1], tab_words[1])
+
+        v_w = [[held([P, BANK], U32, "v_w%d_%d" % (a, jh)) for jh in range(HALVES)] for a in range(PASSES)]
+
+        def gather_v(a):
+            for jh in range(HALVES):
+                cols = slice(jh * BANK // 16, (jh + 1) * BANK // 16)
+                nc.vector.tensor_copy(v_w[a][jh][:], tab_w[a][:].bitcast(U32).indirect(offs_t[:, cols]))
+
+        w4_c = held([P, PACK, PASSES * P * 2], U8, "w4_c")
+        w4_s = held([P, PACK, PASSES * P], U8, "w4_s")
+        nc.vector.tensor_copy(
+            w4_c[:].bitcast(U16).rearrange("p t g -> p g t"),
+            w4_raw[:].rearrange("p a c -> p (a c)").bitcast(U16).rearrange("p (g t) -> p g t", t=PACK),
+        )
+        nc.vector.tensor_copy(v_s[:], tab_s[:].indirect(offs_t[:]))
+        gather_v(0)
+        for a in range(1, PASSES):
+            nc.sync.dma_start(
+                v_s0[a][0:SHIFT_ROWS, :].bitcast(I32), v_s[4 * a : 4 * a + SHIFT_ROWS, :].bitcast(I32),
+            )
+        load_words(tab_w[2], tab_words[2])
+        load_wave(0, 0)
+        nc.sync.dma_start(gain_t[:], gain.rearrange("(p t) -> p t", t=PACK))
+        load_wave(0, 1)
+        load_wave(1, 0)
+        nc.sync.dma_start(offs2_t[:], offs2)
+        for q in range(4):
+            nc.sync.dma_start(
+                tab2_s[32 * q : 32 * q + 4, :].bitcast(I32),
+                tab2_scales[0, 4 * q : 4 * q + 4, :].bitcast(I32),
+            )
+        load_wave(1, 1)
+        load_words(tab2_w, tab2_words[0])
+        nc.sync.dma_start(pos1_t[:], pos1)
+        nc.sync.dma_start(pos2_t[:], pos2)
+        rider_v = rider.rearrange("(i p) n -> p i n", p=P)
+        for u in range(M_TILES // 2):
+            nc.sync.dma_start(rider_t[u][:], rider_v[:, 2 * u : 2 * u + 2, :])
+        with nc.allow_non_contiguous_dma(reason="one value a partition and row tile"):
+            nc.sync.dma_start(hull_t[:], hull.rearrange("(i p) -> p i", p=P))
+
+        w1_c = [held([P, H], U32, "w1_c%d" % a) for a in range(PASSES)]
+        w1_s = [held([P, H], U8, "w1_s%d" % a) for a in range(PASSES)]
+        w1_b = [held([P, PACK, P, PACK], BF16, "w1_b%d" % a) for a in range(PASSES)]
+        for a in range(PASSES):
+            nc.scalar.copy(
+                w1_b[a][:].rearrange("p t m i -> p m i t"),
+                w1_raw[a][:].rearrange("p i (m t) -> p m i t", t=PACK),
+            )
+            nc.vector.quantize_mx(
+                out=w1_c[a][:].bitcast(FP8X4), scales=w1_s[a][:],
+                in_=w1_b[a][:].rearrange("p t m i -> p (t m i)"),
+            )
+        nc.vector.tensor_copy(
+            w4_s[:].rearrange("p t g -> p g t"),
+            w4s_raw[:].rearrange("p a (m t) -> p (a m) t", t=PACK),
+        )
+        gather_v(1)
+        gather_v(2)
+
+        neg_gain = held([P, PACK], F32, "neg_gain")
+        nc.scalar.activation(neg_gain[:], gain_t[:], ACT.Copy, scale=-1.0)
+
+        def mm_a(acc, a, t, jh):
+            cols = slice(t * P, (t + 1) * P)
+            nc.tensor.matmul_mx(
+                out=acc[:], lhsT=w1_c[a][:, cols].bitcast(FP8X4), lhsT_scale=w1_s[a][:, cols],
+                rhs=v_w[a][jh][:].bitcast(FP8X4), rhs_scale=v_s[4 * a : P, jh * BANK : (jh + 1) * BANK],
+                start=(a == 0), stop=(a == PASSES - 1),
+            )
+
+        def mm_b(acc, a, t, jh):
+            nc.tensor.matmul_mx(
+                out=acc[:], lhsT=w4_c[:, t, a * 2 * P : (a + 1) * 2 * P].bitcast(FP4X4),
+                lhsT_scale=w4_s[:, t, a * P : (a + 1) * P],
+                rhs=v_w[a][jh][:].bitcast(FP8X4), rhs_scale=v_s0[a][:, jh * BANK : (jh + 1) * BANK],
+                start=(a == 0), stop=(a == PASSES - 1),
+            )
+
+        h_c = [held([P, BANK], U32, "h_c%d" % jh) for jh in range(HALVES)]
+        h_s = [held([P, BANK], U8, "h_s%d" % jh) for jh in range(HALVES)]
+        v2_w, v2_s = [], []
+
+        def gather_v2_words(cols, tag):
+            words = held([P, 16 * (cols.stop - cols.start)], U32, "v2_w%d" % cols.start, tag)
+            nc.vector.tensor_copy(words[:], tab2_w[:].bitcast(U32).indirect(offs2_t[:, cols]))
+            v2_w.append(words)
+
+        def gather_v2_scales(cols, tag):
+            plane = held([P, 16 * (cols.stop - cols.start)], U8, "v2_s%d" % cols.start, tag)
+            nc.vector.tensor_copy(plane[:], tab2_s[:].indirect(offs2_t[:, cols]))
+            v2_s.append(plane)
+
+        early, late = slice(0, FIRST // 16), slice(FIRST // 16, S2 // 16)
+
+        for jh in range(HALVES):
+            acc_a = [psum.tile([P, BANK], F32, name="acc") for t in range(PACK)]
+            acc_b = [psum.tile([P, BANK], F32, name="acc") for t in range(PACK)]
+            if jh == 0:
+                for a in range(PASSES):
+                    for t in range(PACK):
+                        mm_a(acc_a[t], a, t, jh)
+                    for t in range(PACK):
+                        mm_b(acc_b[t], a, t, jh)
+            else:
+                for t in range(PACK):
+                    for a in range(PASSES):
+                        mm_a(acc_a[t], a, t, jh)
+                for t in range(PACK):
+                    for a in range(PASSES):
+                        mm_b(acc_b[t], a, t, jh)
+            h_b = held([P, PACK, BANK], BF16, "h_b%d" % jh)
+            miss = []
+            for t in range(PACK):
+                diff = held([P, BANK], F32, "diff%d_%d" % (jh, t), "diff%d" % t)
+                nc.vector.tensor_tensor(diff[:], acc_a[t][:], wave_t[jh][t // 2][:, t % 2, :], ALU.subtract)
+
+                miss.append(held([P, BANK], F32, "miss%d_%d" % (jh, t), "miss%d" % t))
+                nc.scalar.activation(miss[t][:], diff[:], ACT.Square)
+            h_i = []
+            for c0 in range(0, BANK, PIECE):
+                cols = slice(c0, c0 + PIECE)
+                for t in range(PACK):
+                    nc.vector.scalar_tensor_tensor(
+                        h_b[:, t, cols], miss[t][:, cols], neg_gain[:, t : t + 1], acc_b[t][:, cols],
+                        ALU.mult, ALU.add,
+                    )
+                h_i.append(held([P, PIECE, PACK], BF16, "h_i%d_%d" % (jh, c0)))
+                nc.scalar.copy(
+                    h_i[-1][:].rearrange("p (c i) t -> p c t i", i=4),
+                    h_b[:, :, cols].rearrange("p t (c i) -> p c t i", i=4),
+                )
+            if jh == HALVES - 1:
+                gather_v2_words(early, None)
+                gather_v2_scales(early, None)
+                gather_v2_words(late, "miss%d" % (PACK - 1))
+            for c0 in range(0, BANK, PIECE):
+                cols = slice(c0, c0 + PIECE)
+                nc.vector.quantize_mx(
+                    out=h_c[jh][:, cols].bitcast(FP8X4), scales=h_s[jh][:, cols],
+                    in_=h_i[c0 // PIECE][:].rearrange("p j t -> p (j t)"),
+                )
+        gather_v2_scales(late, "h_b%d" % (HALVES - 1))
+
+
+        def finish(i, turn_raw, takeoff, tag):
+            res = held([P, NP], F32, "res%d" % i, tag)
+            nc.vector.scalar_tensor_tensor(
+                res[:], turn_raw[:], hull_t[:, i : i + 1], takeoff[:], ALU.max, ALU.subtract, reverse1=True,
+            )
+            nc.sync.dma_start(out[i * P : (i + 1) * P, :], res[:])
+
+        pending = None
+        for i in range(M_TILES):
+            part = 0 if i * P < FIRST else 1
+            cols = slice(i * P - part * FIRST, (i + 1) * P - part * FIRST)
+            e_t = held([P, S], F32, "e%d" % i)
+            for jh in range(HALVES):
+                acc = psum.tile([P, BANK], F32, name="acc")
+                nc.tensor.matmul_mx(
+                    out=acc[:], lhsT=v2_w[part][:, cols].bitcast(FP8X4), lhsT_scale=v2_s[part][:, cols],
+                    rhs=h_c[jh][:].bitcast(FP8X4), rhs_scale=h_s[jh][:], start=True, stop=True,
+                )
+                nc.scalar.copy(e_t[:, jh * BANK : (jh + 1) * BANK], acc[:])
+            g1 = ring.tile([P, NP], F32, name="g1")
+            g2 = ring.tile([P, NP], F32, name="g2")
+            nc.vector.tensor_copy(g1[:], e_t[:].indirect(pos1_t[:]))
+            nc.vector.tensor_copy(g2[:], e_t[:].indirect(pos2_t[:]))
+            if pending is not None:
+                finish(*pending, "e%d" % i)
+            takeoff = ring.tile([P, NP], F32, name="takeoff")
+            nc.vector.tensor_tensor(takeoff[:], g1[:], rider_t[i // 2][:, i % 2, :], ALU.max)
+            pending = (i, g2, takeoff)
+        finish(*pending, None)

@@ -25,6 +25,8 @@ PIECE = 256
 M_TILES = S2 // P
 FIRST = 256
 SHIFT_ROWS = 112
+F32_MAX = 3.4028234663852886e38
+SCALAR_SHARE = 32
 
 
 def tile_list_surfboard_blank_scores_kernel(
@@ -49,7 +51,8 @@ def tile_list_surfboard_blank_scores_kernel(
         tab_s = held([P, T], U8, "tab_s")
         tab2_w = held([P, T], I32, "tab2_w")
         tab2_s = held([P, T], U8, "tab2_s")
-        w1_raw = [held([P, PACK, H], F32, "w1_raw%d" % a) for a in range(PASSES)]
+        w1_raw = [held([P, PACK, H], F32, "w1_raw%d" % a) for a in range(PASSES - 1)]
+        w1_last = [held([P, PACK, H // 2], F32, "w1_last%d" % u) for u in range(2)]
         w4_raw = held([P, PASSES, 2 * H], U8, "w4_raw")
         w4s_raw = held([P, PASSES, H], U8, "w4s_raw")
         wave_t = [[held([P, 2, BANK], F32, "wave%d_%d" % (jh, u)) for u in range(2)] for jh in range(HALVES)]
@@ -59,10 +62,9 @@ def tile_list_surfboard_blank_scores_kernel(
         v_s = held([P, S], U8, "v_s")
         v_s0 = [v_s] + [held([P, S], U8, "v_s%d" % a) for a in range(1, PASSES)]
 
-        nc.gpsimd.memset(tab_s[:].bitcast(I32), 0)
         nc.gpsimd.memset(w4s_raw[:].rearrange("p a c -> p (a c)").bitcast(I32), 0)
-        for plane in (tab2_s, v_s0[1], v_s0[2]):
-            nc.vector.memset(plane[:].bitcast(I32), 0)
+        nc.gpsimd.memset(tab_s[:].bitcast(I32), 0)
+        nc.vector.memset(tab2_s[:].bitcast(I32), 0)
 
         def load_words(dst, words):
             nc.sync.dma_start(dst[:], words.rearrange("p t i -> p (t i)").bitcast(I32))
@@ -77,7 +79,13 @@ def tile_list_surfboard_blank_scores_kernel(
 
         nc.sync.dma_start(offs_t[:], offs)
         nc.sync.dma_start(w4_raw[:].bitcast(I32), w4_words.rearrange("a p c -> p a c").bitcast(I32))
+        for q in range(4):
+            nc.sync.dma_start(
+                w4s_raw[32 * q : 32 * q + 4, :, :].bitcast(I32),
+                w4_scales[:, 4 * q : 4 * q + 4, :].rearrange("a q c -> q a c").bitcast(I32),
+            )
         load_words(tab_w[0], tab_words[0])
+        load_w1(0)
         for q in range(4):
             nc.sync.dma_start(
                 tab_s[32 * q : 32 * q + 4 * PASSES, :].bitcast(I32),
@@ -87,15 +95,13 @@ def tile_list_surfboard_blank_scores_kernel(
         nc.vector.memset(warm[:], 0.0)
         warm2 = held([P, 1], F32, "warm2")
         nc.scalar.activation(warm2[:], warm[:], ACT.Square)
-        load_w1(0)
-        load_w1(1)
-        load_w1(2)
-        for q in range(4):
-            nc.sync.dma_start(
-                w4s_raw[32 * q : 32 * q + 4, :, :].bitcast(I32),
-                w4_scales[:, 4 * q : 4 * q + 4, :].rearrange("a q c -> q a c").bitcast(I32),
-            )
         load_words(tab_w[1], tab_words[1])
+        load_w1(1)
+        load_words(tab_w[2], tab_words[2])
+        last_rows = w1[(PASSES - 1) * P * PACK :, :].rearrange("(p i) r -> p i r", i=PACK)
+        for u in range(2):
+            nc.sync.dma_start(w1_last[u][:], last_rows[:, :, u * H // 2 : (u + 1) * H // 2])
+        load_wave(0, 0)
 
         v_w = [[held([P, BANK], U32, "v_w%d_%d" % (a, jh)) for jh in range(HALVES)] for a in range(PASSES)]
 
@@ -110,14 +116,16 @@ def tile_list_surfboard_blank_scores_kernel(
             w4_c[:].bitcast(U16).rearrange("p t g -> p g t"),
             w4_raw[:].rearrange("p a c -> p (a c)").bitcast(U16).rearrange("p (g t) -> p g t", t=PACK),
         )
-        nc.vector.tensor_copy(v_s[:], tab_s[:].indirect(offs_t[:]))
+        nc.vector.tensor_copy(
+            w4_s[:].rearrange("p t g -> p g t"),
+            w4s_raw[:].rearrange("p a (m t) -> p (a m) t", t=PACK),
+        )
         gather_v(0)
+        nc.vector.tensor_copy(v_s[:], tab_s[:].indirect(offs_t[:]))
         for a in range(1, PASSES):
             nc.sync.dma_start(
                 v_s0[a][0:SHIFT_ROWS, :].bitcast(I32), v_s[4 * a : 4 * a + SHIFT_ROWS, :].bitcast(I32),
             )
-        load_words(tab_w[2], tab_words[2])
-        load_wave(0, 0)
         nc.sync.dma_start(gain_t[:], gain.rearrange("(p t) -> p t", t=PACK))
         load_wave(0, 1)
         load_wave(1, 0)
@@ -140,7 +148,7 @@ def tile_list_surfboard_blank_scores_kernel(
         w1_c = [held([P, H], U32, "w1_c%d" % a) for a in range(PASSES)]
         w1_s = [held([P, H], U8, "w1_s%d" % a) for a in range(PASSES)]
         w1_b = [held([P, PACK, P, PACK], BF16, "w1_b%d" % a) for a in range(PASSES)]
-        for a in range(PASSES):
+        for a in range(PASSES - 1):
             nc.scalar.copy(
                 w1_b[a][:].rearrange("p t m i -> p m i t"),
                 w1_raw[a][:].rearrange("p i (m t) -> p m i t", t=PACK),
@@ -149,12 +157,20 @@ def tile_list_surfboard_blank_scores_kernel(
                 out=w1_c[a][:].bitcast(FP8X4), scales=w1_s[a][:],
                 in_=w1_b[a][:].rearrange("p t m i -> p (t m i)"),
             )
-        nc.vector.tensor_copy(
-            w4_s[:].rearrange("p t g -> p g t"),
-            w4s_raw[:].rearrange("p a (m t) -> p (a m) t", t=PACK),
-        )
         gather_v(1)
         gather_v(2)
+        last = PASSES - 1
+        dealt = w1_b[last][:].rearrange("p t m i -> p m i t")
+        halves = [w1_last[u][:].rearrange("p i (m t) -> p m i t", t=PACK) for u in range(2)]
+        nc.scalar.copy(dealt[:, 0 : P // 2], halves[0])
+        nc.scalar.copy(dealt[:, P // 2 : P // 2 + SCALAR_SHARE], halves[1][:, 0:SCALAR_SHARE])
+        nc.vector.tensor_copy(dealt[:, P // 2 + SCALAR_SHARE : P], halves[1][:, SCALAR_SHARE : P // 2])
+        for t in range(PACK):
+            cols = slice(t * P, (t + 1) * P)
+            nc.vector.quantize_mx(
+                out=w1_c[last][:, cols].bitcast(FP8X4), scales=w1_s[last][:, cols],
+                in_=w1_b[last][:, t].rearrange("p m i -> p (m i)"),
+            )
 
         neg_gain = held([P, PACK], F32, "neg_gain")
         nc.scalar.activation(neg_gain[:], gain_t[:], ACT.Copy, scale=-1.0)
@@ -215,6 +231,9 @@ def tile_list_surfboard_blank_scores_kernel(
 
                 miss.append(held([P, BANK], F32, "miss%d_%d" % (jh, t), "miss%d" % t))
                 nc.scalar.activation(miss[t][:], diff[:], ACT.Square)
+            if jh == HALVES - 1:
+                gather_v2_scales(early, "wave%d_0" % jh)
+                gather_v2_words(early, "wave%d_1" % jh)
             h_i = []
             for c0 in range(0, BANK, PIECE):
                 cols = slice(c0, c0 + PIECE)
@@ -229,8 +248,6 @@ def tile_list_surfboard_blank_scores_kernel(
                     h_b[:, :, cols].rearrange("p t (c i) -> p c t i", i=4),
                 )
             if jh == HALVES - 1:
-                gather_v2_words(early, None)
-                gather_v2_scales(early, None)
                 gather_v2_words(late, "miss%d" % (PACK - 1))
             for c0 in range(0, BANK, PIECE):
                 cols = slice(c0, c0 + PIECE)
@@ -262,11 +279,13 @@ def tile_list_surfboard_blank_scores_kernel(
                 nc.scalar.copy(e_t[:, jh * BANK : (jh + 1) * BANK], acc[:])
             g1 = ring.tile([P, NP], F32, name="g1")
             g2 = ring.tile([P, NP], F32, name="g2")
-            nc.vector.tensor_copy(g1[:], e_t[:].indirect(pos1_t[:]))
             nc.vector.tensor_copy(g2[:], e_t[:].indirect(pos2_t[:]))
-            if pending is not None:
-                finish(*pending, "e%d" % i)
+            nc.vector.tensor_copy(g1[:], e_t[:].indirect(pos1_t[:]))
             takeoff = ring.tile([P, NP], F32, name="takeoff")
+            res = ring.tile([P, NP], F32, name="res")
+            turn = ring.tile([P, NP], F32, name="turn")
+            nc.gpsimd.tensor_scalar(turn[:], g2[:], F32_MAX, hull_t[:, i : i + 1], ALU.min, ALU.max)
             nc.vector.tensor_tensor(takeoff[:], g1[:], rider_t[i // 2][:, i % 2, :], ALU.max)
-            pending = (i, g2, takeoff)
-        finish(*pending, None)
+            last_step = nc.vector if i == M_TILES - 1 else nc.gpsimd
+            last_step.tensor_tensor(res[:], takeoff[:], turn[:], ALU.subtract)
+            nc.sync.dma_start(out[i * P : (i + 1) * P, :], res[:])

@@ -2,7 +2,7 @@ from contextlib import ExitStack
 
 import concourse.mybir as mybir
 
-K, H, T, S, S2, NP = 1536, 512, 2048, 1024, 1024, 512
+K, H, T, S, S2, PAIRS = 1536, 512, 2048, 1024, 1024, 512
 FLOPS = 2 * (2 * K * H * S + H * S2 * S)
 
 F32 = mybir.dt.float32
@@ -18,15 +18,21 @@ ACT = mybir.ActivationFunctionType
 
 P = 128
 PACK = 4
+QUADS = 4
 PASSES = K // (P * PACK)
 BANK = 512
 HALVES = S // BANK
 PIECE = 256
-M_TILES = S2 // P
-FIRST = 256
+ROW_TILES = S2 // P
+PER_COL = 16
 SHIFT_ROWS = 112
-F32_MAX = 3.4028234663852886e38
 SCALAR_SHARE = 32
+EARLY_WORDS = 256
+EARLY_SCALES = 256
+
+
+def entries(start, stop):
+    return slice(start // PER_COL, stop // PER_COL)
 
 
 def tile_list_surfboard_blank_scores_kernel(
@@ -39,13 +45,13 @@ def tile_list_surfboard_blank_scores_kernel(
         ring = ctx.enter_context(tc.tile_pool(name="ring", bufs=3))
         psum = ctx.enter_context(tc.psum_pool(name="psum", bufs=8))
 
-        def held(shape, dtype, name, tag=None):
-            return keep.tile(shape, dtype, name=name, tag=tag or name, align_bytes=64)
+        def held(shape, dtype, name, after=None):
+            return keep.tile(shape, dtype, name=name, tag=after or name, align_bytes=64)
 
-        offs_t = held([P, S // 16], U16, "offs_t")
-        offs2_t = held([P, S2 // 16], U16, "offs2_t")
-        pos1_t = held([P, NP // 16], U16, "pos1_t")
-        pos2_t = held([P, NP // 16], U16, "pos2_t")
+        offs_t = held([P, S // PER_COL], U16, "offs_t")
+        offs2_t = held([P, S2 // PER_COL], U16, "offs2_t")
+        pos1_t = held([P, PAIRS // PER_COL], U16, "pos1_t")
+        pos2_t = held([P, PAIRS // PER_COL], U16, "pos2_t")
 
         tab_w = [held([P, T], I32, "tab_w%d" % a) for a in range(PASSES)]
         tab_s = held([P, T], U8, "tab_s")
@@ -56,14 +62,13 @@ def tile_list_surfboard_blank_scores_kernel(
         w4_raw = held([P, PASSES, 2 * H], U8, "w4_raw")
         w4s_raw = held([P, PASSES, H], U8, "w4s_raw")
         wave_t = [[held([P, 2, BANK], F32, "wave%d_%d" % (jh, u)) for u in range(2)] for jh in range(HALVES)]
-        rider_t = [held([P, 2, NP], F32, "rider%d" % u) for u in range(M_TILES // 2)]
+        rider_t = [held([P, 2, PAIRS], F32, "rider%d" % u) for u in range(ROW_TILES // 2)]
         gain_t = held([P, PACK], F32, "gain_t")
-        hull_t = held([P, M_TILES], F32, "hull_t")
-        v_s = held([P, S], U8, "v_s")
-        v_s0 = [v_s] + [held([P, S], U8, "v_s%d" % a) for a in range(1, PASSES)]
+        hull_t = held([P, ROW_TILES], F32, "hull_t")
+        v_s = [held([P, S], U8, "v_s%d" % a) for a in range(PASSES)]
 
-        nc.gpsimd.memset(w4s_raw[:].rearrange("p a c -> p (a c)").bitcast(I32), 0)
         nc.gpsimd.memset(tab_s[:].bitcast(I32), 0)
+        nc.vector.memset(w4s_raw[:].rearrange("p a c -> p (a c)").bitcast(I32), 0)
         nc.vector.memset(tab2_s[:].bitcast(I32), 0)
 
         def load_words(dst, words):
@@ -79,36 +84,64 @@ def tile_list_surfboard_blank_scores_kernel(
 
         nc.sync.dma_start(offs_t[:], offs)
         nc.sync.dma_start(w4_raw[:].bitcast(I32), w4_words.rearrange("a p c -> p a c").bitcast(I32))
-        for q in range(4):
-            nc.sync.dma_start(
-                w4s_raw[32 * q : 32 * q + 4, :, :].bitcast(I32),
-                w4_scales[:, 4 * q : 4 * q + 4, :].rearrange("a q c -> q a c").bitcast(I32),
-            )
         load_words(tab_w[0], tab_words[0])
         load_w1(0)
-        for q in range(4):
+        for q in range(QUADS):
             nc.sync.dma_start(
                 tab_s[32 * q : 32 * q + 4 * PASSES, :].bitcast(I32),
                 tab_scales[:, 4 * q : 4 * q + 4, :].bitcast(I32),
             )
-        warm = held([P, 1], F32, "warm")
-        nc.vector.memset(warm[:], 0.0)
-        warm2 = held([P, 1], F32, "warm2")
-        nc.scalar.activation(warm2[:], warm[:], ACT.Square)
         load_words(tab_w[1], tab_words[1])
+        nc.sync.dma_start(offs2_t[:], offs2)
+        for q in range(QUADS):
+            nc.sync.dma_start(
+                w4s_raw[32 * q : 32 * q + 4, :, :].bitcast(I32),
+                w4_scales[:, 4 * q : 4 * q + 4, :].rearrange("a s c -> s a c").bitcast(I32),
+            )
         load_w1(1)
+        for q in range(QUADS):
+            nc.sync.dma_start(
+                tab2_s[32 * q : 32 * q + 4, :].bitcast(I32),
+                tab2_scales[0, 4 * q : 4 * q + 4, :].bitcast(I32),
+            )
         load_words(tab_w[2], tab_words[2])
         last_rows = w1[(PASSES - 1) * P * PACK :, :].rearrange("(p i) r -> p i r", i=PACK)
         for u in range(2):
             nc.sync.dma_start(w1_last[u][:], last_rows[:, :, u * H // 2 : (u + 1) * H // 2])
         load_wave(0, 0)
+        warm_in = held([P, 1], F32, "warm_in")
+        warm_out = held([P, 1], F32, "warm_out")
+        nc.vector.memset(warm_in[:], 0.0)
+        nc.scalar.activation(warm_out[:], warm_in[:], ACT.Square)
 
         v_w = [[held([P, BANK], U32, "v_w%d_%d" % (a, jh)) for jh in range(HALVES)] for a in range(PASSES)]
 
-        def gather_v(a):
-            for jh in range(HALVES):
-                cols = slice(jh * BANK // 16, (jh + 1) * BANK // 16)
-                nc.vector.tensor_copy(v_w[a][jh][:], tab_w[a][:].bitcast(U32).indirect(offs_t[:, cols]))
+        def gather_v(a, jh):
+            picks = offs_t[:, entries(jh * BANK, (jh + 1) * BANK)]
+            nc.vector.tensor_copy(v_w[a][jh][:], tab_w[a][:].bitcast(U32).indirect(picks))
+
+        def gather_v2_words(start, stop, after=None):
+            words = held([P, stop - start], U32, "v2_w%d" % start, after)
+            nc.vector.tensor_copy(words[:], tab2_w[:].bitcast(U32).indirect(offs2_t[:, entries(start, stop)]))
+            return words
+
+        def gather_v2_scales(start, stop, after=None):
+            plane = held([P, stop - start], U8, "v2_s%d" % start, after)
+            nc.vector.tensor_copy(plane[:], tab2_s[:].indirect(offs2_t[:, entries(start, stop)]))
+            return plane
+
+        w1_c = [held([P, H], U32, "w1_c%d" % a) for a in range(PASSES)]
+        w1_s = [held([P, H], U8, "w1_s%d" % a) for a in range(PASSES)]
+
+        def quantise_w1(a):
+            dealt = held([P, PACK, P, PACK], BF16, "w1_b%d" % a)
+            nc.scalar.copy(
+                dealt[:].rearrange("p t m i -> p m i t"),
+                w1_raw[a][:].rearrange("p i (m t) -> p m i t", t=PACK),
+            )
+            nc.vector.quantize_mx(
+                out=w1_c[a][:].bitcast(FP8X4), scales=w1_s[a][:], in_=dealt[:].rearrange("p t m i -> p (t m i)"),
+            )
 
         w4_c = held([P, PACK, PASSES * P * 2], U8, "w4_c")
         w4_s = held([P, PACK, PASSES * P], U8, "w4_s")
@@ -116,96 +149,74 @@ def tile_list_surfboard_blank_scores_kernel(
             w4_c[:].bitcast(U16).rearrange("p t g -> p g t"),
             w4_raw[:].rearrange("p a c -> p (a c)").bitcast(U16).rearrange("p (g t) -> p g t", t=PACK),
         )
-        nc.vector.tensor_copy(
-            w4_s[:].rearrange("p t g -> p g t"),
-            w4s_raw[:].rearrange("p a (m t) -> p (a m) t", t=PACK),
-        )
-        gather_v(0)
-        nc.vector.tensor_copy(v_s[:], tab_s[:].indirect(offs_t[:]))
+        gather_v(0, 0)
+        gather_v(0, 1)
+        nc.vector.tensor_copy(v_s[0][:], tab_s[:].indirect(offs_t[:]))
         for a in range(1, PASSES):
             nc.sync.dma_start(
-                v_s0[a][0:SHIFT_ROWS, :].bitcast(I32), v_s[4 * a : 4 * a + SHIFT_ROWS, :].bitcast(I32),
+                v_s[a][0:SHIFT_ROWS, :].bitcast(I32), v_s[0][4 * a : 4 * a + SHIFT_ROWS, :].bitcast(I32),
             )
         nc.sync.dma_start(gain_t[:], gain.rearrange("(p t) -> p t", t=PACK))
         load_wave(0, 1)
         load_wave(1, 0)
-        nc.sync.dma_start(offs2_t[:], offs2)
-        for q in range(4):
-            nc.sync.dma_start(
-                tab2_s[32 * q : 32 * q + 4, :].bitcast(I32),
-                tab2_scales[0, 4 * q : 4 * q + 4, :].bitcast(I32),
-            )
         load_wave(1, 1)
         load_words(tab2_w, tab2_words[0])
         nc.sync.dma_start(pos1_t[:], pos1)
         nc.sync.dma_start(pos2_t[:], pos2)
-        rider_v = rider.rearrange("(i p) n -> p i n", p=P)
-        for u in range(M_TILES // 2):
-            nc.sync.dma_start(rider_t[u][:], rider_v[:, 2 * u : 2 * u + 2, :])
-        with nc.allow_non_contiguous_dma(reason="one value a partition and row tile"):
+        rider_rows = rider.rearrange("(i p) n -> p i n", p=P)
+        for u in range(ROW_TILES // 2):
+            nc.sync.dma_start(rider_t[u][:], rider_rows[:, 2 * u : 2 * u + 2, :])
+        with nc.allow_non_contiguous_dma(reason="one value for each partition and row tile"):
             nc.sync.dma_start(hull_t[:], hull.rearrange("(i p) -> p i", p=P))
 
-        w1_c = [held([P, H], U32, "w1_c%d" % a) for a in range(PASSES)]
-        w1_s = [held([P, H], U8, "w1_s%d" % a) for a in range(PASSES)]
-        w1_b = [held([P, PACK, P, PACK], BF16, "w1_b%d" % a) for a in range(PASSES)]
-        for a in range(PASSES - 1):
-            nc.scalar.copy(
-                w1_b[a][:].rearrange("p t m i -> p m i t"),
-                w1_raw[a][:].rearrange("p i (m t) -> p m i t", t=PACK),
-            )
-            nc.vector.quantize_mx(
-                out=w1_c[a][:].bitcast(FP8X4), scales=w1_s[a][:],
-                in_=w1_b[a][:].rearrange("p t m i -> p (t m i)"),
-            )
-        gather_v(1)
-        gather_v(2)
+        gather_v(1, 0)
+        gather_v(1, 1)
+        nc.vector.tensor_copy(
+            w4_s[:].rearrange("p t g -> p g t"),
+            w4s_raw[:].rearrange("p a (m t) -> p (a m) t", t=PACK),
+        )
+        quantise_w1(0)
+        early_scales = gather_v2_scales(0, EARLY_SCALES)
+        gather_v(2, 0)
+        gather_v(2, 1)
+        quantise_w1(1)
+
         last = PASSES - 1
-        dealt = w1_b[last][:].rearrange("p t m i -> p m i t")
-        halves = [w1_last[u][:].rearrange("p i (m t) -> p m i t", t=PACK) for u in range(2)]
-        nc.scalar.copy(dealt[:, 0 : P // 2], halves[0])
-        nc.scalar.copy(dealt[:, P // 2 : P // 2 + SCALAR_SHARE], halves[1][:, 0:SCALAR_SHARE])
-        nc.vector.tensor_copy(dealt[:, P // 2 + SCALAR_SHARE : P], halves[1][:, SCALAR_SHARE : P // 2])
+        last_dealt = held([P, PACK, P, PACK], BF16, "last_dealt")
+        into = last_dealt[:].rearrange("p t m i -> p m i t")
+        first, second = [w1_last[u][:].rearrange("p i (m t) -> p m i t", t=PACK) for u in range(2)]
+        nc.scalar.copy(into[:, 0 : P // 2], first)
+        nc.scalar.copy(into[:, P // 2 : P // 2 + SCALAR_SHARE], second[:, 0:SCALAR_SHARE])
+        nc.vector.tensor_copy(into[:, P // 2 + SCALAR_SHARE : P], second[:, SCALAR_SHARE : P // 2])
         for t in range(PACK):
             cols = slice(t * P, (t + 1) * P)
             nc.vector.quantize_mx(
                 out=w1_c[last][:, cols].bitcast(FP8X4), scales=w1_s[last][:, cols],
-                in_=w1_b[last][:, t].rearrange("p m i -> p (m i)"),
+                in_=last_dealt[:, t].rearrange("p m i -> p (m i)"),
             )
 
         neg_gain = held([P, PACK], F32, "neg_gain")
         nc.scalar.activation(neg_gain[:], gain_t[:], ACT.Copy, scale=-1.0)
 
-        def mm_a(acc, a, t, jh):
+        def pass_a(acc, a, t, jh):
             cols = slice(t * P, (t + 1) * P)
             nc.tensor.matmul_mx(
                 out=acc[:], lhsT=w1_c[a][:, cols].bitcast(FP8X4), lhsT_scale=w1_s[a][:, cols],
-                rhs=v_w[a][jh][:].bitcast(FP8X4), rhs_scale=v_s[4 * a : P, jh * BANK : (jh + 1) * BANK],
+                rhs=v_w[a][jh][:].bitcast(FP8X4), rhs_scale=v_s[0][4 * a : P, jh * BANK : (jh + 1) * BANK],
                 start=(a == 0), stop=(a == PASSES - 1),
             )
 
-        def mm_b(acc, a, t, jh):
+        def pass_b(acc, a, t, jh):
             nc.tensor.matmul_mx(
                 out=acc[:], lhsT=w4_c[:, t, a * 2 * P : (a + 1) * 2 * P].bitcast(FP4X4),
                 lhsT_scale=w4_s[:, t, a * P : (a + 1) * P],
-                rhs=v_w[a][jh][:].bitcast(FP8X4), rhs_scale=v_s0[a][:, jh * BANK : (jh + 1) * BANK],
+                rhs=v_w[a][jh][:].bitcast(FP8X4), rhs_scale=v_s[a][:, jh * BANK : (jh + 1) * BANK],
                 start=(a == 0), stop=(a == PASSES - 1),
             )
 
         h_c = [held([P, BANK], U32, "h_c%d" % jh) for jh in range(HALVES)]
         h_s = [held([P, BANK], U8, "h_s%d" % jh) for jh in range(HALVES)]
-        v2_w, v2_s = [], []
-
-        def gather_v2_words(cols, tag):
-            words = held([P, 16 * (cols.stop - cols.start)], U32, "v2_w%d" % cols.start, tag)
-            nc.vector.tensor_copy(words[:], tab2_w[:].bitcast(U32).indirect(offs2_t[:, cols]))
-            v2_w.append(words)
-
-        def gather_v2_scales(cols, tag):
-            plane = held([P, 16 * (cols.stop - cols.start)], U8, "v2_s%d" % cols.start, tag)
-            nc.vector.tensor_copy(plane[:], tab2_s[:].indirect(offs2_t[:, cols]))
-            v2_s.append(plane)
-
-        early, late = slice(0, FIRST // 16), slice(FIRST // 16, S2 // 16)
+        pieces = [slice(c, c + PIECE) for c in range(0, BANK, PIECE)]
 
         for jh in range(HALVES):
             acc_a = [psum.tile([P, BANK], F32, name="acc") for t in range(PACK)]
@@ -213,17 +224,16 @@ def tile_list_surfboard_blank_scores_kernel(
             if jh == 0:
                 for a in range(PASSES):
                     for t in range(PACK):
-                        mm_a(acc_a[t], a, t, jh)
+                        pass_a(acc_a[t], a, t, jh)
                     for t in range(PACK):
-                        mm_b(acc_b[t], a, t, jh)
+                        pass_b(acc_b[t], a, t, jh)
             else:
                 for t in range(PACK):
                     for a in range(PASSES):
-                        mm_a(acc_a[t], a, t, jh)
+                        pass_a(acc_a[t], a, t, jh)
                 for t in range(PACK):
                     for a in range(PASSES):
-                        mm_b(acc_b[t], a, t, jh)
-            h_b = held([P, PACK, BANK], BF16, "h_b%d" % jh)
+                        pass_b(acc_b[t], a, t, jh)
             miss = []
             for t in range(PACK):
                 diff = held([P, BANK], F32, "diff%d_%d" % (jh, t), "diff%d" % t)
@@ -232,60 +242,62 @@ def tile_list_surfboard_blank_scores_kernel(
                 miss.append(held([P, BANK], F32, "miss%d_%d" % (jh, t), "miss%d" % t))
                 nc.scalar.activation(miss[t][:], diff[:], ACT.Square)
             if jh == HALVES - 1:
-                gather_v2_scales(early, "wave%d_0" % jh)
-                gather_v2_words(early, "wave%d_1" % jh)
-            h_i = []
-            for c0 in range(0, BANK, PIECE):
-                cols = slice(c0, c0 + PIECE)
+                early_words = gather_v2_words(0, EARLY_WORDS, "wave%d_0" % jh)
+            h_slots = held([P, PACK, BANK], BF16, "h_slots%d" % jh)
+            h_woven = []
+            for cols in pieces:
                 for t in range(PACK):
                     nc.vector.scalar_tensor_tensor(
-                        h_b[:, t, cols], miss[t][:, cols], neg_gain[:, t : t + 1], acc_b[t][:, cols],
+                        h_slots[:, t, cols], miss[t][:, cols], neg_gain[:, t : t + 1], acc_b[t][:, cols],
                         ALU.mult, ALU.add,
                     )
-                h_i.append(held([P, PIECE, PACK], BF16, "h_i%d_%d" % (jh, c0)))
+                h_woven.append(held([P, PIECE, PACK], BF16, "h_woven%d_%d" % (jh, cols.start)))
                 nc.scalar.copy(
-                    h_i[-1][:].rearrange("p (c i) t -> p c t i", i=4),
-                    h_b[:, :, cols].rearrange("p t (c i) -> p c t i", i=4),
+                    h_woven[-1][:].rearrange("p (c i) t -> p c t i", i=4),
+                    h_slots[:, :, cols].rearrange("p t (c i) -> p c t i", i=4),
                 )
             if jh == HALVES - 1:
-                gather_v2_words(late, "miss%d" % (PACK - 1))
-            for c0 in range(0, BANK, PIECE):
-                cols = slice(c0, c0 + PIECE)
+                late_words = gather_v2_words(EARLY_WORDS, S2, "miss%d" % (PACK - 2))
+            for cols, woven in zip(pieces, h_woven):
                 nc.vector.quantize_mx(
                     out=h_c[jh][:, cols].bitcast(FP8X4), scales=h_s[jh][:, cols],
-                    in_=h_i[c0 // PIECE][:].rearrange("p j t -> p (j t)"),
+                    in_=woven[:].rearrange("p j t -> p (j t)"),
                 )
-        gather_v2_scales(late, "h_b%d" % (HALVES - 1))
+        late_scales = gather_v2_scales(EARLY_SCALES, S2, "h_slots%d" % (HALVES - 1))
 
 
-        def finish(i, turn_raw, takeoff, tag):
-            res = held([P, NP], F32, "res%d" % i, tag)
+        def tile_columns(i, early, late, split):
+            if i * P < split:
+                return early[:, i * P : (i + 1) * P]
+            return late[:, i * P - split : (i + 1) * P - split]
+
+        def finish(i, turn_scores, takeoff, cols, after):
+            result = held([P, cols.stop - cols.start], F32, "result%d_%d" % (i, cols.start), after)
             nc.vector.scalar_tensor_tensor(
-                res[:], turn_raw[:], hull_t[:, i : i + 1], takeoff[:], ALU.max, ALU.subtract, reverse1=True,
+                result[:], turn_scores[:, cols], hull_t[:, i : i + 1], takeoff[:, cols],
+                ALU.max, ALU.subtract, reverse1=True,
             )
-            nc.sync.dma_start(out[i * P : (i + 1) * P, :], res[:])
+            nc.sync.dma_start(out[i * P : (i + 1) * P, cols], result[:])
 
         pending = None
-        for i in range(M_TILES):
-            part = 0 if i * P < FIRST else 1
-            cols = slice(i * P - part * FIRST, (i + 1) * P - part * FIRST)
-            e_t = held([P, S], F32, "e%d" % i)
+        for i in range(ROW_TILES):
+            scores = held([P, S], F32, "scores%d" % i)
             for jh in range(HALVES):
                 acc = psum.tile([P, BANK], F32, name="acc")
                 nc.tensor.matmul_mx(
-                    out=acc[:], lhsT=v2_w[part][:, cols].bitcast(FP8X4), lhsT_scale=v2_s[part][:, cols],
+                    out=acc[:], lhsT=tile_columns(i, early_words, late_words, EARLY_WORDS).bitcast(FP8X4),
+                    lhsT_scale=tile_columns(i, early_scales, late_scales, EARLY_SCALES),
                     rhs=h_c[jh][:].bitcast(FP8X4), rhs_scale=h_s[jh][:], start=True, stop=True,
                 )
-                nc.scalar.copy(e_t[:, jh * BANK : (jh + 1) * BANK], acc[:])
-            g1 = ring.tile([P, NP], F32, name="g1")
-            g2 = ring.tile([P, NP], F32, name="g2")
-            nc.vector.tensor_copy(g2[:], e_t[:].indirect(pos2_t[:]))
-            nc.vector.tensor_copy(g1[:], e_t[:].indirect(pos1_t[:]))
-            takeoff = ring.tile([P, NP], F32, name="takeoff")
-            res = ring.tile([P, NP], F32, name="res")
-            turn = ring.tile([P, NP], F32, name="turn")
-            nc.gpsimd.tensor_scalar(turn[:], g2[:], F32_MAX, hull_t[:, i : i + 1], ALU.min, ALU.max)
-            nc.vector.tensor_tensor(takeoff[:], g1[:], rider_t[i // 2][:, i % 2, :], ALU.max)
-            last_step = nc.vector if i == M_TILES - 1 else nc.gpsimd
-            last_step.tensor_tensor(res[:], takeoff[:], turn[:], ALU.subtract)
-            nc.sync.dma_start(out[i * P : (i + 1) * P, :], res[:])
+                nc.scalar.copy(scores[:, jh * BANK : (jh + 1) * BANK], acc[:])
+            takeoff_scores = ring.tile([P, PAIRS], F32, name="takeoff_scores")
+            turn_scores = ring.tile([P, PAIRS], F32, name="turn_scores")
+            nc.vector.tensor_copy(takeoff_scores[:], scores[:].indirect(pos1_t[:]))
+            nc.vector.tensor_copy(turn_scores[:], scores[:].indirect(pos2_t[:]))
+            takeoff = ring.tile([P, PAIRS], F32, name="takeoff")
+            nc.vector.tensor_tensor(takeoff[:], takeoff_scores[:], rider_t[i // 2][:, i % 2, :], ALU.max)
+            if pending is not None:
+                finish(*pending, slice(0, PAIRS), "scores%d" % i)
+            pending = (i, turn_scores, takeoff)
+        for half in range(2):
+            finish(*pending, slice(half * PAIRS // 2, (half + 1) * PAIRS // 2), None)

@@ -1,6 +1,7 @@
 from contextlib import ExitStack
 
 import concourse.mybir as mybir
+from concourse.masks import make_identity
 
 K, H, T, S, S2, PAIRS = 1536, 512, 2048, 1024, 1024, 512
 FLOPS = 2 * (2 * K * H * S + H * S2 * S)
@@ -27,6 +28,8 @@ ROW_TILES = S2 // P
 PER_COL = 16
 SHIFT_ROWS = 112
 SCALAR_SHARE = 32
+TENSOR_TILES = 6
+SCORES_AHEAD = 2
 EARLY_WORDS = 256
 EARLY_SCALES = 256
 
@@ -85,25 +88,25 @@ def tile_list_surfboard_blank_scores_kernel(
         nc.sync.dma_start(offs_t[:], offs)
         nc.sync.dma_start(w4_raw[:].bitcast(I32), w4_words.rearrange("a p c -> p a c").bitcast(I32))
         load_words(tab_w[0], tab_words[0])
-        load_w1(0)
+        nc.sync.dma_start(offs2_t[:], offs2)
         for q in range(QUADS):
             nc.sync.dma_start(
                 tab_s[32 * q : 32 * q + 4 * PASSES, :].bitcast(I32),
                 tab_scales[:, 4 * q : 4 * q + 4, :].bitcast(I32),
             )
-        load_words(tab_w[1], tab_words[1])
-        nc.sync.dma_start(offs2_t[:], offs2)
+        load_w1(0)
         for q in range(QUADS):
             nc.sync.dma_start(
                 w4s_raw[32 * q : 32 * q + 4, :, :].bitcast(I32),
                 w4_scales[:, 4 * q : 4 * q + 4, :].rearrange("a s c -> s a c").bitcast(I32),
             )
-        load_w1(1)
+        load_words(tab_w[1], tab_words[1])
         for q in range(QUADS):
             nc.sync.dma_start(
                 tab2_s[32 * q : 32 * q + 4, :].bitcast(I32),
                 tab2_scales[0, 4 * q : 4 * q + 4, :].bitcast(I32),
             )
+        load_w1(1)
         load_words(tab_w[2], tab_words[2])
         last_rows = w1[(PASSES - 1) * P * PACK :, :].rearrange("(p i) r -> p i r", i=PACK)
         for u in range(2):
@@ -279,9 +282,32 @@ def tile_list_surfboard_blank_scores_kernel(
             )
             nc.sync.dma_start(out[i * P : (i + 1) * P, cols], result[:])
 
-        pending = None
-        for i in range(ROW_TILES):
-            scores = held([P, S], F32, "scores%d" % i)
+        identity = held([P, P], F32, "identity")
+        make_identity(nc, identity[:])
+
+        def add_turned(takeoff, neg_turn):
+            turned_sum = psum.tile([P, PAIRS], F32, name="acc")
+            for c in range(0, PAIRS, P):
+                for term, opens in ((takeoff, True), (neg_turn, False)):
+                    nc.tensor.matmul(
+                        turned_sum[:, c : c + P], term[:, c : c + P], identity[:],
+                        start=opens, stop=not opens, is_transpose=True,
+                    )
+            turned = ring.tile([P, PAIRS], F32, name="turned", bufs=2)
+            nc.scalar.copy(turned[:], turned_sum[:])
+            return turned
+
+        def turn_back(i, turned):
+            upright = psum.tile([P, PAIRS], F32, name="acc")
+            for c in range(0, PAIRS, P):
+                nc.tensor.transpose(upright[:, c : c + P], turned[:, c : c + P], identity[:])
+            result = held([P, PAIRS], F32, "result%d" % i, "scores%d" % i)
+            nc.scalar.copy(result[:], upright[:])
+            nc.sync.dma_start(out[i * P : (i + 1) * P, :], result[:])
+
+        scores = [held([P, S], F32, "scores%d" % i) for i in range(ROW_TILES)]
+
+        def make_scores(i):
             for jh in range(HALVES):
                 acc = psum.tile([P, BANK], F32, name="acc")
                 nc.tensor.matmul_mx(
@@ -289,13 +315,30 @@ def tile_list_surfboard_blank_scores_kernel(
                     lhsT_scale=tile_columns(i, early_scales, late_scales, EARLY_SCALES),
                     rhs=h_c[jh][:].bitcast(FP8X4), rhs_scale=h_s[jh][:], start=True, stop=True,
                 )
-                nc.scalar.copy(scores[:, jh * BANK : (jh + 1) * BANK], acc[:])
+                nc.scalar.copy(scores[i][:, jh * BANK : (jh + 1) * BANK], acc[:])
+
+        for i in range(SCORES_AHEAD):
+            make_scores(i)
+        turned = None
+        pending = None
+        for i in range(ROW_TILES):
+            if i + SCORES_AHEAD < ROW_TILES:
+                make_scores(i + SCORES_AHEAD)
             takeoff_scores = ring.tile([P, PAIRS], F32, name="takeoff_scores")
             turn_scores = ring.tile([P, PAIRS], F32, name="turn_scores")
-            nc.vector.tensor_copy(takeoff_scores[:], scores[:].indirect(pos1_t[:]))
-            nc.vector.tensor_copy(turn_scores[:], scores[:].indirect(pos2_t[:]))
+            nc.vector.tensor_copy(takeoff_scores[:], scores[i][:].indirect(pos1_t[:]))
+            nc.vector.tensor_copy(turn_scores[:], scores[i][:].indirect(pos2_t[:]))
             takeoff = ring.tile([P, PAIRS], F32, name="takeoff")
             nc.vector.tensor_tensor(takeoff[:], takeoff_scores[:], rider_t[i // 2][:, i % 2, :], ALU.max)
+            if i < TENSOR_TILES:
+                neg_turn = ring.tile([P, PAIRS], F32, name="neg_turn", bufs=2)
+                nc.vector.tensor_scalar(neg_turn[:], turn_scores[:], hull_t[:, i : i + 1], -1.0, ALU.max, ALU.mult)
+                turned, earlier = add_turned(takeoff, neg_turn), turned
+                if i > 0:
+                    turn_back(i - 1, earlier)
+                if i == TENSOR_TILES - 1:
+                    turn_back(i, turned)
+                continue
             if pending is not None:
                 finish(*pending, slice(0, PAIRS), "scores%d" % i)
             pending = (i, turn_scores, takeoff)

from contextlib import ExitStack

import concourse.mybir as mybir
from concourse.masks import make_identity

K, H, T, S, S2, PAIRS = 1536, 512, 2048, 1024, 1024, 512
FLOPS = 2 * (2 * K * H * S + H * S2 * S)

F32 = mybir.dt.float32
BF16 = mybir.dt.bfloat16
I32 = mybir.dt.int32
U32 = mybir.dt.uint32
U16 = mybir.dt.uint16
U8 = mybir.dt.uint8
FP8X4 = mybir.dt.float8_e4m3fn_x4
FP4X4 = mybir.dt.float4_e2m1fn_x4
ALU = mybir.AluOpType
ACT = mybir.ActivationFunctionType

P = 128
PACK = 4
QUADS = 4
PASSES = K // (P * PACK)
BANK = 512
HALVES = S // BANK
PIECE = 256
ROW_TILES = S2 // P
PER_COL = 16
SHIFT_ROWS = 112
SCALAR_SHARE = 32
TENSOR_TILES = 6
SCORES_AHEAD = 2
EARLY_WORDS = 256
EARLY_SCALES = 256


def entries(start, stop):
    return slice(start // PER_COL, stop // PER_COL)


def tile_list_surfboard_blank_scores_kernel(
    tc, tab_words, tab_scales, tab2_words, tab2_scales, offs, offs2, pos1, pos2,
    w1, w4_words, w4_scales, wave, gain, rider, hull, out,
):
    nc = tc.nc
    with ExitStack() as ctx:
        keep = ctx.enter_context(tc.tile_pool(name="keep", bufs=1))
        ring = ctx.enter_context(tc.tile_pool(name="ring", bufs=3))
        psum = ctx.enter_context(tc.psum_pool(name="psum", bufs=8))

        def held(shape, dtype, name, after=None):
            return keep.tile(shape, dtype, name=name, tag=after or name, align_bytes=64)

        offs_t = held([P, S // PER_COL], U16, "offs_t")
        offs2_t = held([P, S2 // PER_COL], U16, "offs2_t")
        pos1_t = held([P, PAIRS // PER_COL], U16, "pos1_t")
        pos2_t = held([P, PAIRS // PER_COL], U16, "pos2_t")

        tab_w = [held([P, T], I32, "tab_w%d" % a) for a in range(PASSES)]
        tab_s = held([P, T], U8, "tab_s")
        tab2_w = held([P, T], I32, "tab2_w")
        tab2_s = held([P, T], U8, "tab2_s")
        w1_raw = [held([P, PACK, H], F32, "w1_raw%d" % a) for a in range(PASSES - 1)]
        w1_last = [held([P, PACK, H // 2], F32, "w1_last%d" % u) for u in range(2)]
        w4_raw = held([P, PASSES, 2 * H], U8, "w4_raw")
        w4s_raw = held([P, PASSES, H], U8, "w4s_raw")
        wave_t = [[held([P, 2, BANK], F32, "wave%d_%d" % (jh, u)) for u in range(2)] for jh in range(HALVES)]
        rider_t = [held([P, 2, PAIRS], F32, "rider%d" % u) for u in range(ROW_TILES // 2)]
        gain_t = held([P, PACK], F32, "gain_t")
        hull_t = held([P, ROW_TILES], F32, "hull_t")
        v_s = [held([P, S], U8, "v_s%d" % a) for a in range(PASSES)]

        nc.gpsimd.memset(tab_s[:].bitcast(I32), 0)
        nc.vector.memset(w4s_raw[:].rearrange("p a c -> p (a c)").bitcast(I32), 0)
        nc.vector.memset(tab2_s[:].bitcast(I32), 0)

        def load_words(dst, words):
            nc.sync.dma_start(dst[:], words.rearrange("p t i -> p (t i)").bitcast(I32))

        def load_w1(a):
            rows = w1[a * P * PACK : (a + 1) * P * PACK, :]
            nc.sync.dma_start(w1_raw[a][:], rows.rearrange("(p i) r -> p i r", i=PACK))

        def load_wave(jh, u):
            src = wave.rearrange("(p t) j -> p t j", t=PACK)
            nc.sync.dma_start(wave_t[jh][u][:], src[:, 2 * u : 2 * u + 2, jh * BANK : (jh + 1) * BANK])

        nc.sync.dma_start(offs_t[:], offs)
        nc.sync.dma_start(w4_raw[:].bitcast(I32), w4_words.rearrange("a p c -> p a c").bitcast(I32))
        load_words(tab_w[0], tab_words[0])
        nc.sync.dma_start(offs2_t[:], offs2)
        for q in range(QUADS):
            nc.sync.dma_start(
                tab_s[32 * q : 32 * q + 4 * PASSES, :].bitcast(I32),
                tab_scales[:, 4 * q : 4 * q + 4, :].bitcast(I32),
            )
        load_w1(0)
        for q in range(QUADS):
            nc.sync.dma_start(
                w4s_raw[32 * q : 32 * q + 4, :, :].bitcast(I32),
                w4_scales[:, 4 * q : 4 * q + 4, :].rearrange("a s c -> s a c").bitcast(I32),
            )
        load_words(tab_w[1], tab_words[1])
        for q in range(QUADS):
            nc.sync.dma_start(
                tab2_s[32 * q : 32 * q + 4, :].bitcast(I32),
                tab2_scales[0, 4 * q : 4 * q + 4, :].bitcast(I32),
            )
        load_w1(1)
        load_words(tab_w[2], tab_words[2])
        last_rows = w1[(PASSES - 1) * P * PACK :, :].rearrange("(p i) r -> p i r", i=PACK)
        for u in range(2):
            nc.sync.dma_start(w1_last[u][:], last_rows[:, :, u * H // 2 : (u + 1) * H // 2])
        load_wave(0, 0)
        warm_in = held([P, 1], F32, "warm_in")
        warm_out = held([P, 1], F32, "warm_out")
        nc.vector.memset(warm_in[:], 0.0)
        nc.scalar.activation(warm_out[:], warm_in[:], ACT.Square)

        v_w = [[held([P, BANK], U32, "v_w%d_%d" % (a, jh)) for jh in range(HALVES)] for a in range(PASSES)]

        def gather_v(a, jh):
            picks = offs_t[:, entries(jh * BANK, (jh + 1) * BANK)]
            nc.vector.tensor_copy(v_w[a][jh][:], tab_w[a][:].bitcast(U32).indirect(picks))

        def gather_v2_words(start, stop, after=None):
            words = held([P, stop - start], U32, "v2_w%d" % start, after)
            nc.vector.tensor_copy(words[:], tab2_w[:].bitcast(U32).indirect(offs2_t[:, entries(start, stop)]))
            return words

        def gather_v2_scales(start, stop, after=None):
            plane = held([P, stop - start], U8, "v2_s%d" % start, after)
            nc.vector.tensor_copy(plane[:], tab2_s[:].indirect(offs2_t[:, entries(start, stop)]))
            return plane

        w1_c = [held([P, H], U32, "w1_c%d" % a) for a in range(PASSES)]
        w1_s = [held([P, H], U8, "w1_s%d" % a) for a in range(PASSES)]

        def quantise_w1(a):
            dealt = held([P, PACK, P, PACK], BF16, "w1_b%d" % a)
            nc.scalar.copy(
                dealt[:].rearrange("p t m i -> p m i t"),
                w1_raw[a][:].rearrange("p i (m t) -> p m i t", t=PACK),
            )
            nc.vector.quantize_mx(
                out=w1_c[a][:].bitcast(FP8X4), scales=w1_s[a][:], in_=dealt[:].rearrange("p t m i -> p (t m i)"),
            )

        w4_c = held([P, PACK, PASSES * P * 2], U8, "w4_c")
        w4_s = held([P, PACK, PASSES * P], U8, "w4_s")
        nc.vector.tensor_copy(
            w4_c[:].bitcast(U16).rearrange("p t g -> p g t"),
            w4_raw[:].rearrange("p a c -> p (a c)").bitcast(U16).rearrange("p (g t) -> p g t", t=PACK),
        )
        gather_v(0, 0)
        gather_v(0, 1)
        nc.vector.tensor_copy(v_s[0][:], tab_s[:].indirect(offs_t[:]))
        for a in range(1, PASSES):
            nc.sync.dma_start(
                v_s[a][0:SHIFT_ROWS, :].bitcast(I32), v_s[0][4 * a : 4 * a + SHIFT_ROWS, :].bitcast(I32),
            )
        nc.sync.dma_start(gain_t[:], gain.rearrange("(p t) -> p t", t=PACK))
        load_wave(0, 1)
        load_wave(1, 0)
        load_wave(1, 1)
        load_words(tab2_w, tab2_words[0])
        nc.sync.dma_start(pos1_t[:], pos1)
        nc.sync.dma_start(pos2_t[:], pos2)
        rider_rows = rider.rearrange("(i p) n -> p i n", p=P)
        for u in range(ROW_TILES // 2):
            nc.sync.dma_start(rider_t[u][:], rider_rows[:, 2 * u : 2 * u + 2, :])
        with nc.allow_non_contiguous_dma(reason="one value for each partition and row tile"):
            nc.sync.dma_start(hull_t[:], hull.rearrange("(i p) -> p i", p=P))

        gather_v(1, 0)
        gather_v(1, 1)
        nc.vector.tensor_copy(
            w4_s[:].rearrange("p t g -> p g t"),
            w4s_raw[:].rearrange("p a (m t) -> p (a m) t", t=PACK),
        )
        quantise_w1(0)
        early_scales = gather_v2_scales(0, EARLY_SCALES)
        gather_v(2, 0)
        gather_v(2, 1)
        quantise_w1(1)

        last = PASSES - 1
        last_dealt = held([P, PACK, P, PACK], BF16, "last_dealt")
        into = last_dealt[:].rearrange("p t m i -> p m i t")
        first, second = [w1_last[u][:].rearrange("p i (m t) -> p m i t", t=PACK) for u in range(2)]
        nc.scalar.copy(into[:, 0 : P // 2], first)
        nc.scalar.copy(into[:, P // 2 : P // 2 + SCALAR_SHARE], second[:, 0:SCALAR_SHARE])
        nc.vector.tensor_copy(into[:, P // 2 + SCALAR_SHARE : P], second[:, SCALAR_SHARE : P // 2])
        for t in range(PACK):
            cols = slice(t * P, (t + 1) * P)
            nc.vector.quantize_mx(
                out=w1_c[last][:, cols].bitcast(FP8X4), scales=w1_s[last][:, cols],
                in_=last_dealt[:, t].rearrange("p m i -> p (m i)"),
            )

        neg_gain = held([P, PACK], F32, "neg_gain")
        nc.scalar.activation(neg_gain[:], gain_t[:], ACT.Copy, scale=-1.0)

        def pass_a(acc, a, t, jh):
            cols = slice(t * P, (t + 1) * P)
            nc.tensor.matmul_mx(
                out=acc[:], lhsT=w1_c[a][:, cols].bitcast(FP8X4), lhsT_scale=w1_s[a][:, cols],
                rhs=v_w[a][jh][:].bitcast(FP8X4), rhs_scale=v_s[0][4 * a : P, jh * BANK : (jh + 1) * BANK],
                start=(a == 0), stop=(a == PASSES - 1),
            )

        def pass_b(acc, a, t, jh):
            nc.tensor.matmul_mx(
                out=acc[:], lhsT=w4_c[:, t, a * 2 * P : (a + 1) * 2 * P].bitcast(FP4X4),
                lhsT_scale=w4_s[:, t, a * P : (a + 1) * P],
                rhs=v_w[a][jh][:].bitcast(FP8X4), rhs_scale=v_s[a][:, jh * BANK : (jh + 1) * BANK],
                start=(a == 0), stop=(a == PASSES - 1),
            )

        h_c = [held([P, BANK], U32, "h_c%d" % jh) for jh in range(HALVES)]
        h_s = [held([P, BANK], U8, "h_s%d" % jh) for jh in range(HALVES)]
        pieces = [slice(c, c + PIECE) for c in range(0, BANK, PIECE)]

        for jh in range(HALVES):
            acc_a = [psum.tile([P, BANK], F32, name="acc") for t in range(PACK)]
            acc_b = [psum.tile([P, BANK], F32, name="acc") for t in range(PACK)]
            if jh == 0:
                for a in range(PASSES):
                    for t in range(PACK):
                        pass_a(acc_a[t], a, t, jh)
                    for t in range(PACK):
                        pass_b(acc_b[t], a, t, jh)
            else:
                for t in range(PACK):
                    for a in range(PASSES):
                        pass_a(acc_a[t], a, t, jh)
                for t in range(PACK):
                    for a in range(PASSES):
                        pass_b(acc_b[t], a, t, jh)
            miss = []
            for t in range(PACK):
                diff = held([P, BANK], F32, "diff%d_%d" % (jh, t), "diff%d" % t)
                nc.vector.tensor_tensor(diff[:], acc_a[t][:], wave_t[jh][t // 2][:, t % 2, :], ALU.subtract)

                miss.append(held([P, BANK], F32, "miss%d_%d" % (jh, t), "miss%d" % t))
                nc.scalar.activation(miss[t][:], diff[:], ACT.Square)
            if jh == HALVES - 1:
                early_words = gather_v2_words(0, EARLY_WORDS, "wave%d_0" % jh)
            h_slots = held([P, PACK, BANK], BF16, "h_slots%d" % jh)
            h_woven = []
            for cols in pieces:
                for t in range(PACK):
                    nc.vector.scalar_tensor_tensor(
                        h_slots[:, t, cols], miss[t][:, cols], neg_gain[:, t : t + 1], acc_b[t][:, cols],
                        ALU.mult, ALU.add,
                    )
                h_woven.append(held([P, PIECE, PACK], BF16, "h_woven%d_%d" % (jh, cols.start)))
                nc.scalar.copy(
                    h_woven[-1][:].rearrange("p (c i) t -> p c t i", i=4),
                    h_slots[:, :, cols].rearrange("p t (c i) -> p c t i", i=4),
                )
            if jh == HALVES - 1:
                late_words = gather_v2_words(EARLY_WORDS, S2, "miss%d" % (PACK - 2))
            for cols, woven in zip(pieces, h_woven):
                nc.vector.quantize_mx(
                    out=h_c[jh][:, cols].bitcast(FP8X4), scales=h_s[jh][:, cols],
                    in_=woven[:].rearrange("p j t -> p (j t)"),
                )
        late_scales = gather_v2_scales(EARLY_SCALES, S2, "h_slots%d" % (HALVES - 1))


        def tile_columns(i, early, late, split):
            if i * P < split:
                return early[:, i * P : (i + 1) * P]
            return late[:, i * P - split : (i + 1) * P - split]

        def finish(i, turn_scores, takeoff, cols, after):
            result = held([P, cols.stop - cols.start], F32, "result%d_%d" % (i, cols.start), after)
            nc.vector.scalar_tensor_tensor(
                result[:], turn_scores[:, cols], hull_t[:, i : i + 1], takeoff[:, cols],
                ALU.max, ALU.subtract, reverse1=True,
            )
            nc.sync.dma_start(out[i * P : (i + 1) * P, cols], result[:])

        identity = held([P, P], F32, "identity")
        make_identity(nc, identity[:])

        def add_turned(takeoff, neg_turn):
            turned_sum = psum.tile([P, PAIRS], F32, name="acc")
            for c in range(0, PAIRS, P):
                for term, opens in ((takeoff, True), (neg_turn, False)):
                    nc.tensor.matmul(
                        turned_sum[:, c : c + P], term[:, c : c + P], identity[:],
                        start=opens, stop=not opens, is_transpose=True,
                    )
            turned = ring.tile([P, PAIRS], F32, name="turned", bufs=2)
            nc.scalar.copy(turned[:], turned_sum[:])
            return turned

        def turn_back(i, turned):
            upright = psum.tile([P, PAIRS], F32, name="acc")
            for c in range(0, PAIRS, P):
                nc.tensor.transpose(upright[:, c : c + P], turned[:, c : c + P], identity[:])
            result = held([P, PAIRS], F32, "result%d" % i, "scores%d" % i)
            nc.scalar.copy(result[:], upright[:])
            nc.sync.dma_start(out[i * P : (i + 1) * P, :], result[:])

        scores = [held([P, S], F32, "scores%d" % i) for i in range(ROW_TILES)]

        def make_scores(i):
            for jh in range(HALVES):
                acc = psum.tile([P, BANK], F32, name="acc")
                nc.tensor.matmul_mx(
                    out=acc[:], lhsT=tile_columns(i, early_words, late_words, EARLY_WORDS).bitcast(FP8X4),
                    lhsT_scale=tile_columns(i, early_scales, late_scales, EARLY_SCALES),
                    rhs=h_c[jh][:].bitcast(FP8X4), rhs_scale=h_s[jh][:], start=True, stop=True,
                )
                nc.scalar.copy(scores[i][:, jh * BANK : (jh + 1) * BANK], acc[:])

        for i in range(SCORES_AHEAD):
            make_scores(i)
        turned = None
        pending = None
        for i in range(ROW_TILES):
            if i + SCORES_AHEAD < ROW_TILES:
                make_scores(i + SCORES_AHEAD)
            takeoff_scores = ring.tile([P, PAIRS], F32, name="takeoff_scores")
            turn_scores = ring.tile([P, PAIRS], F32, name="turn_scores")
            nc.vector.tensor_copy(takeoff_scores[:], scores[i][:].indirect(pos1_t[:]))
            nc.vector.tensor_copy(turn_scores[:], scores[i][:].indirect(pos2_t[:]))
            takeoff = ring.tile([P, PAIRS], F32, name="takeoff")
            nc.vector.tensor_tensor(takeoff[:], takeoff_scores[:], rider_t[i // 2][:, i % 2, :], ALU.max)
            if i < TENSOR_TILES:
                neg_turn = ring.tile([P, PAIRS], F32, name="neg_turn", bufs=2)
                nc.vector.tensor_scalar(neg_turn[:], turn_scores[:], hull_t[:, i : i + 1], -1.0, ALU.max, ALU.mult)
                turned, earlier = add_turned(takeoff, neg_turn), turned
                if i > 0:
                    turn_back(i - 1, earlier)
                if i == TENSOR_TILES - 1:
                    turn_back(i, turned)
                continue
            if pending is not None:
                finish(*pending, slice(0, PAIRS), "scores%d" % i)
            pending = (i, turn_scores, takeoff)
        for half in range(2):
            finish(*pending, slice(half * PAIRS // 2, (half + 1) * PAIRS // 2), None)
